import numpy as np
import ml_dtypes


def mxq(x, axis, fmt="e4m3"):
    dtype, down = {"e4m3": (ml_dtypes.float8_e4m3fn, 7), "e5m2": (ml_dtypes.float8_e5m2, 14)}[fmt]
    v = np.moveaxis(np.asarray(x, np.float32).astype(ml_dtypes.bfloat16).astype(np.float64), axis, -1)
    blocks = v.reshape(v.shape[:-1] + (-1, 32))
    amax = np.abs(blocks).max(-1, keepdims=True)
    byte = np.maximum(np.where(amax > 0, np.frexp(amax)[1] - 1 + 127, 0) - down, 1)
    scale = np.exp2(byte - 127.0)
    codes = (blocks / scale).astype(np.float32).astype(dtype).astype(np.float64)
    return np.moveaxis((codes * scale).reshape(v.shape), -1, axis)


WIDE = False


def mx_kscale(k):
    if not WIDE:
        return np.ones(k)
    levels = np.array([10, -10, 5, -5, 0])
    if k % 512:
        return np.exp2(np.random.permutation(np.resize(levels, k // 32))).repeat(32)
    a = np.empty((k // 512, 16))
    for p in range(k // 512):
        a[p, :8] = np.random.permutation(np.resize(levels, 8))
        for g in range(8):
            far = levels[np.abs(levels - a[p, g]) >= 10]
            a[p, g + 8] = far[np.random.randint(len(far))]
    return np.exp2(a.ravel()).repeat(32)


BF16 = ml_dtypes.bfloat16


def bf(x):
    return np.asarray(x, np.float32).astype(BF16)


def f64(x):
    return np.asarray(x).astype(np.float64)


E2M1 = np.array([0.0, 0.5, 1.0, 1.5, 2.0, 3.0, 4.0, 6.0, -0.0, -0.5, -1.0, -1.5, -2.0, -3.0, -4.0, -6.0])


def pack_weight(w, fmt):
    k, n = w.shape
    w = f64(bf(w)).reshape(k // 32, 32, n)
    amax = np.abs(w).max(1)
    if fmt == "e4m3":
        byte = np.frexp(amax)[1] - 1 + 127 - 7
    else:
        mant, ex = np.frexp(amax / 6.0)
        byte = np.where(mant > 0.5, ex, ex - 1) + 127
    byte = np.clip(np.where(amax > 0, byte, 1), 1, 254)
    scaled = (w * np.exp2(127.0 - byte)[:, None, :]).reshape(k, n).astype(np.float32)
    by_word = np.ascontiguousarray(scaled.reshape(k // 512, 128, 4, n).transpose(0, 1, 3, 2))
    if fmt == "e4m3":
        words = by_word.astype(ml_dtypes.float8_e4m3fn).view(np.uint8)
    else:
        c = by_word.astype(ml_dtypes.float4_e2m1fn).view(np.uint8) & 0xF
        words = c[..., 0::2] | (c[..., 1::2] << 4)
    return np.ascontiguousarray(words), np.ascontiguousarray(byte.astype(np.uint8).reshape(k // 512, 16, n))


def unpack_weight(words, scales, fmt):
    g, p, n, _ = words.shape
    if fmt == "e4m3":
        vals = np.ascontiguousarray(words).view(ml_dtypes.float8_e4m3fn).astype(np.float64)
    else:
        nib = np.empty((g, p, n, 4), np.uint8)
        nib[..., 0::2] = words & 0xF
        nib[..., 1::2] = words >> 4
        vals = E2M1[nib]
    vals = vals * np.repeat(np.exp2(scales.astype(np.float64) - 127.0), 8, axis=1)[..., None]
    return vals.transpose(0, 1, 3, 2).reshape(g * 512, n)
def pack4(w):
    words, scales = pack_weight(w, "e2m1")
    return words.reshape(words.shape[0], 128, -1), scales


def unpack4(words, scales):
    return unpack_weight(words.reshape(words.shape[0], 128, -1, 2), scales, "e2m1")


def planes(Y):
    n, m = Y.shape
    b = f64(bf(Y)).reshape(n // 32, 32, m)
    amax = np.abs(b).max(1)
    byte = np.clip(np.where(amax > 0, np.frexp(amax)[1] - 1 + 127 - 7, 1), 1, 254)
    codes = (b * np.exp2(127.0 - byte)[:, None, :]).reshape(n, m).astype(np.float32).astype(ml_dtypes.float8_e4m3fn).view(np.uint8)
    words = codes.reshape(n // 512, 128, 4, m).transpose(0, 1, 3, 2)
    return np.ascontiguousarray(words), np.ascontiguousarray(byte.astype(np.uint8).reshape(n // 512, 16, m))


N, F, H, K, C = 1024, 16, 512, 128, 512
FK = F * K


def setup_inputs():
    t = mx_kscale(H)
    r = mx_kscale(FK)
    x = bf(np.random.standard_normal((N, F)))
    a = bf(np.random.standard_normal(H))
    b = bf(np.random.standard_normal(H) * 0.5)
    g = bf(np.random.standard_normal(H) * t)
    w_words, w_scales = pack4(np.random.standard_normal((H, K)) * (2.0 / np.sqrt(H)) / t[:, None])
    s = bf(np.random.standard_normal((F, K)) * r.reshape(F, K))
    v_words, v_scales = pack4(np.random.standard_normal((FK, C)) / np.sqrt(FK) / r[:, None])
    return {
        "x": x,
        "a": a,
        "b": b,
        "g": g,
        "w_words": w_words,
        "w_scales": w_scales,
        "s": s,
        "v_words": v_words,
        "v_scales": v_scales,
    }


def shared_basis(x, a, b, g, w):
    u = np.maximum(a * x[:, :, None] + b, 0.0) * g
    z = mxq(u, 2, "e4m3") @ w
    return np.maximum(z, 0.0)


def core(x, a, b, g, w_words, w_scales, s, v_words, v_scales):
    z = shared_basis(f64(x), f64(a), f64(b), f64(g), unpack4(w_words, w_scales))
    v = unpack4(v_words, v_scales)
    q = (z * f64(s)[None, :, :]).reshape(x.shape[0], v.shape[0])
    return mxq(q, 1, "e4m3") @ v


def reference(x, a, b, g, w_words, w_scales, s, v_words, v_scales):
    R_out = core(x, a, b, g, w_words, w_scales, s, v_words, v_scales)
    words, scales = planes(R_out)
    return R_out, words, scales

@@ -1,0 +1,347 @@
+from contextlib import ExitStack
+
+import concourse.mybir as mybir
+from concourse.masks import make_identity
+
+F32 = mybir.dt.float32
+BF16 = mybir.dt.bfloat16
+I32 = mybir.dt.int32
+U32 = mybir.dt.uint32
+U8 = mybir.dt.uint8
+FP8X4 = mybir.dt.float8_e4m3fn_x4
+FP4X4 = mybir.dt.float4_e2m1fn_x4
+ALU = mybir.AluOpType
+
+N, F, H, K, C = 1024, 16, 512, 128, 512
+FLOPS = 2 * N * F * H * K + 2 * N * F * K * C
+
+P = 128
+BIG = 3.0e38
+UNITS = 16
+N_PE = 2
+SCRATCH = N - UNITS
+
+
+def tile_neuralbasismodelsharedshapes_x2_kernel(
+    tc, x, a, b, g, w_words, w_scales, s, v_words, v_scales, out_0, out_1, out_2
+):
+    nc = tc.nc
+    with ExitStack() as ctx:
+        keep = ctx.enter_context(tc.tile_pool(name="keep", bufs=1))
+        xpool = ctx.enter_context(tc.tile_pool(name="xpool", bufs=UNITS // 2))
+        ypool = ctx.enter_context(tc.tile_pool(name="ypool", bufs=3))
+        upool = ctx.enter_context(tc.tile_pool(name="upool", bufs=4))
+        cpool = ctx.enter_context(tc.tile_pool(name="cpool", bufs=3))
+        qpool = ctx.enter_context(tc.tile_pool(name="qpool", bufs=3))
+        qcpool = ctx.enter_context(tc.tile_pool(name="qcpool", bufs=4))
+        opool = ctx.enter_context(tc.tile_pool(name="opool", bufs=2))
+        zps = ctx.enter_context(tc.psum_pool(name="zps", bufs=4))
+        ops = ctx.enter_context(tc.psum_pool(name="ops", bufs=1))
+        ctx.enter_context(tc.manual_schedule())
+
+        xs = keep.tile([P, 2, 4, F], BF16)
+        nc.sync.dma_start(out=xs[:], in_=x.rearrange("(G p t) f -> p G t f", G=2, t=4))
+        a_sb = keep.tile([P, 4], BF16)
+        b_sb = keep.tile([P, 4], BF16)
+        g_sb = keep.tile([P, 4], BF16)
+        s_sb = keep.tile([P, 4, 4], BF16)
+        nc.scalar.dma_start(out=g_sb[:], in_=g.rearrange("(p t) -> p t", t=4))
+        nc.scalar.dma_start(out=a_sb[:], in_=a.rearrange("(p t) -> p t", t=4))
+        nc.scalar.dma_start(out=b_sb[:], in_=b.rearrange("(p t) -> p t", t=4))
+        nc.scalar.dma_start(
+            out=s_sb[:], in_=s.rearrange("f k -> (f k)").rearrange("(g p t) -> p g t", p=P, t=4)
+        )
+        ident = keep.tile([P, P], BF16)
+        make_identity(nc, ident[:])
+
+        wraw = keep.tile([P, 2 * K], U8, align_bytes=64)
+        wsraw = keep.tile([P, K], U8, align_bytes=64)
+        wz = keep.tile([P, 4, 4, 2 * P], U8, align_bytes=64)
+        wsp = keep.tile([P, 4, 4, 32], U8, align_bytes=64)
+        vt = keep.tile([P, 4, 2 * C], U8, align_bytes=64)
+        vs = keep.tile([P, 4, C], U8, align_bytes=64)
+        nc.vector.memset(wsraw[:].bitcast(I32), 0)
+        nc.vector.memset(wz[:].rearrange("p t j c -> p (t j c)").bitcast(I32), 0)
+        nc.gpsimd.memset(vs[:].rearrange("p g n -> p (g n)").bitcast(I32), 0)
+        nc.sync.dma_start(out=wraw[:].bitcast(I32), in_=w_words[0].bitcast(I32))
+        for Q in range(4):
+            nc.sync.dma_start(
+                out=wsraw[32 * Q : 32 * Q + 4, :].bitcast(I32),
+                in_=w_scales[0, 4 * Q : 4 * Q + 4, :].bitcast(I32),
+            )
+
+        ga = keep.tile([P, 4], F32)
+        gb = keep.tile([P, 4], F32)
+        lo = keep.tile([P, 4], F32)
+        hi = keep.tile([P, 4], F32)
+        nc.vector.tensor_scalar(out=lo[:], in0=g_sb[:], scalar1=0.0, scalar2=-BIG, op0=ALU.is_lt, op1=ALU.mult)
+        nc.vector.tensor_scalar(out=hi[:], in0=g_sb[:], scalar1=0.0, scalar2=BIG, op0=ALU.is_gt, op1=ALU.mult)
+        nc.vector.tensor_tensor(out=ga[:], in0=g_sb[:], in1=a_sb[:], op=ALU.mult)
+        nc.vector.tensor_tensor(out=gb[:], in0=g_sb[:], in1=b_sb[:], op=ALU.mult)
+
+        def unit(u):
+            return u // 8, (u // 4) % 2, u % 4
+
+        xb = []
+        for m in range(N_PE):
+            xu = xpool.tile([P, 2, 1024], BF16, tag="xu", name="xu")
+            xb.append(xu)
+            for e in range(2):
+                G, half, gg = unit(2 * m + e)
+                zx = zps.tile([P, 2, 4, P], BF16, tag="z", name="zx")
+                for tt in range(2):
+                    for j in range(4):
+                        f = 4 * gg + j
+                        nc.tensor.transpose(
+                            zx[:, tt, j, :],
+                            xs[:, G, 2 * half + tt, f : f + 1].to_broadcast([P, P]),
+                            ident[:],
+                        )
+                nc.scalar.copy(out=xu[:, e, :], in_=zx[:].rearrange("p t j n -> p (t j n)"))
+
+        xp = keep.tile([P, 2, 2, 4, 2, 4], BF16)
+        for G in range(2):
+            for half in range(2):
+                nc.vector.tensor_copy(
+                    out=xp[:, G, half],
+                    in_=xs[:, G, 2 * half : 2 * half + 2, :].rearrange("p t (g j) -> p g t j", j=4),
+                )
+        zt = zps.tile([P, P], BF16, tag="z", name="zt")
+        nc.tensor.transpose(zt[:], xp[:].rearrange("p G h g t j -> p (G h g t j)"), ident[:])
+        xt = keep.tile([P, P], BF16)
+        nc.scalar.copy(out=xt[:], in_=zt[:])
+        park = out_0[SCRATCH:N, :].bitcast(BF16)
+        nc.sync.dma_start(out=park.rearrange("u (c n) -> (u c) n", n=P), in_=xt[:])
+        for m in range(N_PE, UNITS // 2):
+            xu = xpool.tile([P, 2, 1024], BF16, tag="xu", name="xu")
+            nc.sync.dma_start(
+                out=xu[:].rearrange("p e c -> p (e c)"),
+                in_=park[2 * m : 2 * m + 2, :].rearrange("u c -> (u c)").partition_broadcast(P),
+            )
+            xb.append(xu)
+
+        nc.sync.dma_start(
+            out=vt[:].rearrange("p g n -> p (g n)").bitcast(I32).rearrange("p (g n) -> p g n", g=4),
+            in_=v_words.bitcast(I32).rearrange("g p n -> p g n"),
+        )
+        for Q in range(4):
+            nc.sync.dma_start(
+                out=vs[32 * Q : 32 * Q + 4, :, :].rearrange("p g n -> p (g n)").bitcast(I32).rearrange("p (g n) -> p g n", g=4),
+                in_=v_scales.bitcast(I32)[:, 4 * Q : 4 * Q + 4, :].rearrange("g r n -> r g n"),
+            )
+
+        ys, us, ucs, zs, qs, qcs, acc, of, ob, oqs = {}, {}, {}, {}, {}, {}, {}, {}, {}, {}
+
+        def affine(m, c0=0, c1=2048):
+            if m not in ys:
+                y = ypool.tile([P, 4, 2048], BF16, name="y")
+                ys[m] = y
+            xin = xb[m][:].rearrange("p e c -> p (e c)")
+            for t in range(4):
+                nc.vector.tensor_scalar(
+                    out=ys[m][:, t, c0:c1], in0=xin[:, c0:c1], scalar1=ga[:, t : t + 1], scalar2=gb[:, t : t + 1],
+                    op0=ALU.mult, op1=ALU.add,
+                )
+
+        def clamp(m, c0=0, c1=2048):
+            for t in range(4):
+                nc.vector.tensor_scalar(
+                    out=ys[m][:, t, c0:c1], in0=ys[m][:, t, c0:c1], scalar1=lo[:, t : t + 1], scalar2=hi[:, t : t + 1],
+                    op0=ALU.max, op1=ALU.min,
+                )
+
+        def interleave(k):
+            u = upool.tile([P, 1024, 4], BF16, name="u", align_bytes=64)
+            us[k] = u
+            y = ys[k // 2]
+            for h in range(2):
+                y0 = 1024 * (k % 2) + 512 * h
+                nc.scalar.copy(
+                    out=u[:, 512 * h : 512 * h + 512, :].rearrange("p (c i) t -> p c t i", i=4),
+                    in_=y[:, :, y0 : y0 + 512].rearrange("p t (c i) -> p c t i", i=4),
+                )
+
+        def quant_u(k, parts=1):
+            codes = cpool.tile([P, 1024], U32, name="codes", align_bytes=64)
+            scales = cpool.tile([P, 1024], U8, name="scales", align_bytes=64)
+            ucs[k] = (codes, scales)
+            w = 1024 // parts
+            for i in range(parts):
+                cols = slice(w * i, w * i + w)
+                nc.vector.quantize_mx(
+                    out=codes[:, cols].bitcast(FP8X4),
+                    scales=scales[:, cols],
+                    in_=us[k][:, cols, :].rearrange("p c t -> p (c t)"),
+                )
+
+        def stage1(k):
+            codes, scales = ucs[k]
+            for tt in range(2):
+                z = zps.tile([P, 4, P], F32, tag="z", name="z")
+                zs[k, tt] = z
+                for t in range(4):
+                    for j in range(4):
+                        cols = slice(512 * tt + 128 * j, 512 * tt + 128 * j + 128)
+                        nc.tensor.matmul_mx(
+                            out=z[:, t, :],
+                            lhsT=wz[:, t, j, :].bitcast(FP4X4),
+                            lhsT_scale=wsp[:, t, :, :].rearrange("p j m -> p (j m)"),
+                            rhs=codes[:, cols].bitcast(FP8X4),
+                            rhs_scale=scales[:, cols],
+                            start=(j == 0),
+                            stop=(j == 3),
+                        )
+
+        def relu_s(k, tt):
+            gg = unit(k)[2]
+            if tt == 0:
+                q = qpool.tile([P, 256, 4], BF16, name="q", align_bytes=64)
+                qs[k] = q
+            nc.vector.scalar_tensor_tensor(
+                out=qs[k][:, 128 * tt : 128 * tt + 128, :],
+                in0=zs[k, tt][:].rearrange("p t n -> p n t"),
+                scalar=0.0,
+                in1=s_sb[:, gg, :].unsqueeze(1).to_broadcast([P, P, 4]),
+                op0=ALU.max,
+                op1=ALU.mult,
+            )
+
+        def quant_q(k, n0=0, n1=256):
+            if k not in qcs:
+                qc = qcpool.tile([P, 256], U32, name="qc", align_bytes=64)
+                qsc = qcpool.tile([P, 256], U8, name="qsc", align_bytes=64)
+                qcs[k] = (qc, qsc)
+            qc, qsc = qcs[k]
+            nc.vector.quantize_mx(
+                out=qc[:, n0:n1].bitcast(FP8X4),
+                scales=qsc[:, n0:n1],
+                in_=qs[k][:, n0:n1, :].rearrange("p c t -> p (c t)"),
+            )
+
+        def stage2(k, tts=(0, 1)):
+            G, half, gg = unit(k)
+            qc, qsc = qcs[k]
+            for tt in tts:
+                t = 2 * half + tt
+                if gg == 0:
+                    o = ops.tile([P, C], F32, tag="o%d" % t, name="o")
+                    acc[G, t] = o
+                cols = slice(128 * tt, 128 * tt + 128)
+                nc.tensor.matmul_mx(
+                    out=acc[G, t][:],
+                    lhsT=qc[:, cols].bitcast(FP8X4),
+                    lhsT_scale=qsc[:, cols],
+                    rhs=vt[:, gg, :].bitcast(FP4X4),
+                    rhs_scale=vs[:, gg, :],
+                    start=(gg == 0),
+                    stop=(gg == 3),
+                )
+
+        def copy_out(G, t, parts=1):
+            if t == 0:
+                o32 = opool.tile([P, 4, C], F32, name="o32")
+                of[G] = o32
+            w = C // parts
+            for i in range(parts):
+                nc.scalar.copy(out=of[G][:, t, w * i : w * i + w], in_=acc[G, t][:, w * i : w * i + w])
+            nc.sync.dma_start(
+                out=out_0[512 * G : 512 * G + 512, :].rearrange("(p t) c -> p t c", t=4)[:, t, :],
+                in_=of[G][:, t, :],
+            )
+
+        def round_out(G, c0=0, c1=C):
+            if G not in ob:
+                o16 = opool.tile([P, C, 4], BF16, name="o16", align_bytes=64)
+                ob[G] = o16
+            nc.vector.tensor_copy(out=ob[G][:, c0:c1, :], in_=of[G][:, :, c0:c1].rearrange("p t c -> p c t"))
+
+        def quant_out(G, c0=0, c1=C):
+            if G not in oqs:
+                oc = opool.tile([P, C], U32, name="oc", align_bytes=64)
+                osc = opool.tile([P, C], U8, name="osc", align_bytes=64)
+                oqs[G] = (oc, osc)
+            oc, osc = oqs[G]
+            nc.vector.quantize_mx(
+                out=oc[:, c0:c1].bitcast(FP8X4),
+                scales=osc[:, c0:c1],
+                in_=ob[G][:, c0:c1, :].rearrange("p c t -> p (c t)"),
+            )
+
+        def store_planes(G):
+            oc, osc = oqs[G]
+            nc.sync.dma_start(
+                out=out_1[G].rearrange("p m t -> p (m t)").bitcast(I32), in_=oc[:].bitcast(I32)
+            )
+            for Q in range(4):
+                nc.sync.dma_start(
+                    out=out_2[G, 4 * Q : 4 * Q + 4, :].bitcast(I32),
+                    in_=osc[32 * Q : 32 * Q + 4, :].bitcast(I32),
+                )
+
+        affine(0, 0, 1024)
+        clamp(0, 0, 1024)
+        interleave(0)
+        affine(0, 1024, 2048)
+        clamp(0, 1024, 2048)
+        interleave(1)
+        for j in range(4):
+            nc.vector.tensor_copy(
+                out=wz[:, :, j, 64 * j : 64 * j + 64].rearrange("p t (m b) -> p t m b", b=2),
+                in_=wraw[:].rearrange("p (m t b) -> p t m b", t=4, b=2),
+            )
+            nc.vector.tensor_copy(
+                out=wsp[:, :, j, :], in_=wsraw[:].rearrange("p (m t) -> p t m", t=4)
+            )
+        affine(1)
+        clamp(1)
+        interleave(2)
+        interleave(3)
+
+        for m in range(8):
+            k = 2 * m
+            if m + 2 < 8:
+                affine(m + 2)
+            if m > 0:
+                quant_q(k - 2)
+                stage2(k - 2)
+            quant_u(k)
+            stage1(k)
+            if m > 0:
+                relu_s(k - 1, 0)
+                relu_s(k - 1, 1)
+            if m + 2 < 8:
+                clamp(m + 2)
+                interleave(k + 4)
+            if m in (3, 5, 7):
+                G, half = (m - 3) // 4, ((m - 3) // 2) % 2
+                copy_out(G, 2 * half)
+                copy_out(G, 2 * half + 1)
+            if m + 2 < 8:
+                interleave(k + 5)
+            if m > 0:
+                quant_q(k - 1)
+                stage2(k - 1)
+            quant_u(k + 1, 2 if m == 7 else 1)
+            stage1(k + 1)
+            if m == 6:
+                round_out(0)
+            relu_s(k, 0)
+            relu_s(k, 1)
+            if m == 6:
+                quant_out(0)
+                store_planes(0)
+        relu_s(15, 0)
+        quant_q(14)
+        stage2(14)
+        quant_q(15, 0, 128)
+        stage2(15, (0,))
+        copy_out(1, 2)
+        relu_s(15, 1)
+        quant_q(15, 128, 256)
+        stage2(15, (1,))
+        copy_out(1, 3, 2)
+        round_out(1, 0, 256)
+        round_out(1, 256, 512)
+        quant_out(1, 0, 256)
+        quant_out(1, 256, 512)
+        store_planes(1)

@@ -18,6 +18,7 @@ FLOPS = 2 * N * F * H * K + 2 * N * F * K * C
 P = 128
 BIG = 3.0e38
 UNITS = 16
+V_CHUNKS = ((7, 1), (11, 1), (15, 1))
 N_PE = 2
 SCRATCH = N - UNITS
 
@@ -30,7 +31,7 @@ def tile_neuralbasismodelsharedshapes_x2_kernel(
         keep = ctx.enter_context(tc.tile_pool(name="keep", bufs=1))
         xpool = ctx.enter_context(tc.tile_pool(name="xpool", bufs=UNITS // 2))
         ypool = ctx.enter_context(tc.tile_pool(name="ypool", bufs=3))
-        upool = ctx.enter_context(tc.tile_pool(name="upool", bufs=4))
+        upool = ctx.enter_context(tc.tile_pool(name="upool", bufs=5))
         cpool = ctx.enter_context(tc.tile_pool(name="cpool", bufs=3))
         qpool = ctx.enter_context(tc.tile_pool(name="qpool", bufs=3))
         qcpool = ctx.enter_context(tc.tile_pool(name="qcpool", bufs=4))
@@ -97,7 +98,13 @@ def tile_neuralbasismodelsharedshapes_x2_kernel(
                             xs[:, G, 2 * half + tt, f : f + 1].to_broadcast([P, P]),
                             ident[:],
                         )
-                nc.scalar.copy(out=xu[:, e, :], in_=zx[:].rearrange("p t j n -> p (t j n)"))
+                parts = 2 if (m, e) == (0, 0) else 1
+                w = 1024 // parts
+                for i in range(parts):
+                    nc.scalar.copy(
+                        out=xu[:, e, w * i : w * i + w],
+                        in_=zx[:].rearrange("p t j n -> p (t j n)")[:, w * i : w * i + w],
+                    )
 
         xp = keep.tile([P, 2, 2, 4, 2, 4], BF16)
         for G in range(2):
@@ -155,11 +162,19 @@ def tile_neuralbasismodelsharedshapes_x2_kernel(
             us[k] = u
             y = ys[k // 2]
             for h in range(2):
-                y0 = 1024 * (k % 2) + 512 * h
-                nc.scalar.copy(
-                    out=u[:, 512 * h : 512 * h + 512, :].rearrange("p (c i) t -> p c t i", i=4),
-                    in_=y[:, :, y0 : y0 + 512].rearrange("p t (c i) -> p c t i", i=4),
-                )
+                if (k, h) not in V_CHUNKS:
+                    y0 = 1024 * (k % 2) + 512 * h
+                    nc.scalar.copy(
+                        out=u[:, 512 * h : 512 * h + 512, :].rearrange("p (c i) t -> p c t i", i=4),
+                        in_=y[:, :, y0 : y0 + 512].rearrange("p t (c i) -> p c t i", i=4),
+                    )
+
+        def interleave_v(k, h):
+            y0 = 1024 * (k % 2) + 512 * h
+            nc.vector.tensor_copy(
+                out=us[k][:, 512 * h : 512 * h + 512, :].rearrange("p (c i) t -> p c t i", i=4),
+                in_=ys[k // 2][:, :, y0 : y0 + 512].rearrange("p t (c i) -> p c t i", i=4),
+            )
 
         def quant_u(k, parts=1):
             codes = cpool.tile([P, 1024], U32, name="codes", align_bytes=64)
@@ -278,8 +293,10 @@ def tile_neuralbasismodelsharedshapes_x2_kernel(
                     in_=osc[32 * Q : 32 * Q + 4, :].bitcast(I32),
                 )
 
-        affine(0, 0, 1024)
-        clamp(0, 0, 1024)
+        affine(0, 0, 512)
+        clamp(0, 0, 512)
+        affine(0, 512, 1024)
+        clamp(0, 512, 1024)
         interleave(0)
         affine(0, 1024, 2048)
         clamp(0, 1024, 2048)
@@ -323,6 +340,9 @@ def tile_neuralbasismodelsharedshapes_x2_kernel(
                 stage2(k - 1)
             quant_u(k + 1, 2 if m == 7 else 1)
             stage1(k + 1)
+            for h in range(2):
+                if (k + 5, h) in V_CHUNKS:
+                    interleave_v(k + 5, h)
             if m == 6:
                 round_out(0)
             relu_s(k, 0)

@@ -18,7 +18,6 @@ FLOPS = 2 * N * F * H * K + 2 * N * F * K * C
 P = 128
 BIG = 3.0e38
 UNITS = 16
-V_CHUNKS = ((7, 1), (11, 1), (15, 1))
 N_PE = 2
 SCRATCH = N - UNITS
 
@@ -41,7 +40,8 @@ def tile_neuralbasismodelsharedshapes_x2_kernel(
         ctx.enter_context(tc.manual_schedule())
 
         xs = keep.tile([P, 2, 4, F], BF16)
-        nc.sync.dma_start(out=xs[:], in_=x.rearrange("(G p t) f -> p G t f", G=2, t=4))
+        x_view = x.rearrange("(G p t) f -> p G t f", G=2, t=4)
+        nc.sync.dma_start(out=xs[:, 0], in_=x_view[:, 0])
         a_sb = keep.tile([P, 4], BF16)
         b_sb = keep.tile([P, 4], BF16)
         g_sb = keep.tile([P, 4], BF16)
@@ -49,22 +49,25 @@ def tile_neuralbasismodelsharedshapes_x2_kernel(
         nc.scalar.dma_start(out=g_sb[:], in_=g.rearrange("(p t) -> p t", t=4))
         nc.scalar.dma_start(out=a_sb[:], in_=a.rearrange("(p t) -> p t", t=4))
         nc.scalar.dma_start(out=b_sb[:], in_=b.rearrange("(p t) -> p t", t=4))
-        nc.scalar.dma_start(
-            out=s_sb[:], in_=s.rearrange("f k -> (f k)").rearrange("(g p t) -> p g t", p=P, t=4)
-        )
+        nc.sync.dma_start(out=xs[:, 1], in_=x_view[:, 1])
         ident = keep.tile([P, P], BF16)
         make_identity(nc, ident[:])
 
         wraw = keep.tile([P, 2 * K], U8, align_bytes=64)
         wsraw = keep.tile([P, K], U8, align_bytes=64)
         wz = keep.tile([P, 4, 4, 2 * P], U8, align_bytes=64)
+        wperm = keep.tile([P, 4, 64], U8, align_bytes=64)
+        wsperm = keep.tile([P, 4, 32], U8, align_bytes=64)
         wsp = keep.tile([P, 4, 4, 32], U8, align_bytes=64)
         vt = keep.tile([P, 4, 2 * C], U8, align_bytes=64)
         vs = keep.tile([P, 4, C], U8, align_bytes=64)
-        nc.vector.memset(wsraw[:].bitcast(I32), 0)
+        nc.gpsimd.memset(wsraw[:].bitcast(I32), 0)
         nc.vector.memset(wz[:].rearrange("p t j c -> p (t j c)").bitcast(I32), 0)
         nc.gpsimd.memset(vs[:].rearrange("p g n -> p (g n)").bitcast(I32), 0)
         nc.sync.dma_start(out=wraw[:].bitcast(I32), in_=w_words[0].bitcast(I32))
+        nc.scalar.dma_start(
+            out=s_sb[:], in_=s.rearrange("f k -> (f k)").rearrange("(g p t) -> p g t", p=P, t=4)
+        )
         for Q in range(4):
             nc.sync.dma_start(
                 out=wsraw[32 * Q : 32 * Q + 4, :].bitcast(I32),
@@ -82,6 +85,22 @@ def tile_neuralbasismodelsharedshapes_x2_kernel(
 
         def unit(u):
             return u // 8, (u // 4) % 2, u % 4
+
+        xp = keep.tile([P, 2, 2, 4, 2, 4], BF16)
+        for G in range(2):
+            for half in range(2):
+                nc.gpsimd.tensor_copy(
+                    out=xp[:, G, half],
+                    in_=xs[:, G, 2 * half : 2 * half + 2, :].rearrange("p t (g j) -> p g t j", j=4),
+                )
+        park = out_0[SCRATCH:N, :].bitcast(BF16)
+
+        def park_x():
+            zt = zps.tile([P, P], BF16, tag="z", name="zt")
+            nc.tensor.transpose(zt[:], xp[:].rearrange("p G h g t j -> p (G h g t j)"), ident[:])
+            xt = keep.tile([P, P], BF16)
+            nc.scalar.copy(out=xt[:], in_=zt[:])
+            nc.sync.dma_start(out=park.rearrange("u (c n) -> (u c) n", n=P), in_=xt[:])
 
         xb = []
         for m in range(N_PE):
@@ -105,20 +124,9 @@ def tile_neuralbasismodelsharedshapes_x2_kernel(
                         out=xu[:, e, w * i : w * i + w],
                         in_=zx[:].rearrange("p t j n -> p (t j n)")[:, w * i : w * i + w],
                     )
+                if (m, e) == (0, 0):
+                    park_x()
 
-        xp = keep.tile([P, 2, 2, 4, 2, 4], BF16)
-        for G in range(2):
-            for half in range(2):
-                nc.vector.tensor_copy(
-                    out=xp[:, G, half],
-                    in_=xs[:, G, 2 * half : 2 * half + 2, :].rearrange("p t (g j) -> p g t j", j=4),
-                )
-        zt = zps.tile([P, P], BF16, tag="z", name="zt")
-        nc.tensor.transpose(zt[:], xp[:].rearrange("p G h g t j -> p (G h g t j)"), ident[:])
-        xt = keep.tile([P, P], BF16)
-        nc.scalar.copy(out=xt[:], in_=zt[:])
-        park = out_0[SCRATCH:N, :].bitcast(BF16)
-        nc.sync.dma_start(out=park.rearrange("u (c n) -> (u c) n", n=P), in_=xt[:])
         for m in range(N_PE, UNITS // 2):
             xu = xpool.tile([P, 2, 1024], BF16, tag="xu", name="xu")
             nc.sync.dma_start(
@@ -139,21 +147,22 @@ def tile_neuralbasismodelsharedshapes_x2_kernel(
 
         ys, us, ucs, zs, qs, qcs, acc, of, ob, oqs = {}, {}, {}, {}, {}, {}, {}, {}, {}, {}
 
-        def affine(m, c0=0, c1=2048):
+        def affine(m, part=None):
             if m not in ys:
-                y = ypool.tile([P, 4, 2048], BF16, name="y")
+                y = ypool.tile([P, 2, 4, 1024], BF16, name="y")
                 ys[m] = y
-            xin = xb[m][:].rearrange("p e c -> p (e c)")
+            e, c = part if part else (slice(0, 2), slice(0, 1024))
             for t in range(4):
                 nc.vector.tensor_scalar(
-                    out=ys[m][:, t, c0:c1], in0=xin[:, c0:c1], scalar1=ga[:, t : t + 1], scalar2=gb[:, t : t + 1],
+                    out=ys[m][:, e, t, c], in0=xb[m][:, e, c], scalar1=ga[:, t : t + 1], scalar2=gb[:, t : t + 1],
                     op0=ALU.mult, op1=ALU.add,
                 )
 
-        def clamp(m, c0=0, c1=2048):
+        def clamp(m, part=None):
+            e, c = part if part else (slice(0, 2), slice(0, 1024))
             for t in range(4):
                 nc.vector.tensor_scalar(
-                    out=ys[m][:, t, c0:c1], in0=ys[m][:, t, c0:c1], scalar1=lo[:, t : t + 1], scalar2=hi[:, t : t + 1],
+                    out=ys[m][:, e, t, c], in0=ys[m][:, e, t, c], scalar1=lo[:, t : t + 1], scalar2=hi[:, t : t + 1],
                     op0=ALU.max, op1=ALU.min,
                 )
 
@@ -162,19 +171,11 @@ def tile_neuralbasismodelsharedshapes_x2_kernel(
             us[k] = u
             y = ys[k // 2]
             for h in range(2):
-                if (k, h) not in V_CHUNKS:
-                    y0 = 1024 * (k % 2) + 512 * h
-                    nc.scalar.copy(
-                        out=u[:, 512 * h : 512 * h + 512, :].rearrange("p (c i) t -> p c t i", i=4),
-                        in_=y[:, :, y0 : y0 + 512].rearrange("p t (c i) -> p c t i", i=4),
-                    )
-
-        def interleave_v(k, h):
-            y0 = 1024 * (k % 2) + 512 * h
-            nc.vector.tensor_copy(
-                out=us[k][:, 512 * h : 512 * h + 512, :].rearrange("p (c i) t -> p c t i", i=4),
-                in_=ys[k // 2][:, :, y0 : y0 + 512].rearrange("p t (c i) -> p c t i", i=4),
-            )
+                y0 = 512 * h
+                nc.scalar.copy(
+                    out=u[:, 512 * h : 512 * h + 512, :].rearrange("p (c i) t -> p c t i", i=4),
+                    in_=y[:, k % 2, :, y0 : y0 + 512].rearrange("p t (c i) -> p c t i", i=4),
+                )
 
         def quant_u(k, parts=1):
             codes = cpool.tile([P, 1024], U32, name="codes", align_bytes=64)
@@ -293,22 +294,25 @@ def tile_neuralbasismodelsharedshapes_x2_kernel(
                     in_=osc[32 * Q : 32 * Q + 4, :].bitcast(I32),
                 )
 
-        affine(0, 0, 512)
-        clamp(0, 0, 512)
-        affine(0, 512, 1024)
-        clamp(0, 512, 1024)
+        for part in ((0, slice(0, 512)), (0, slice(512, 1024))):
+            affine(0, part)
+            clamp(0, part)
         interleave(0)
-        affine(0, 1024, 2048)
-        clamp(0, 1024, 2048)
+        affine(0, (1, slice(0, 1024)))
+        clamp(0, (1, slice(0, 1024)))
         interleave(1)
+        nc.vector.tensor_copy(
+            out=wperm[:].rearrange("p t (m b) -> p t m b", b=2),
+            in_=wraw[:].rearrange("p (m t b) -> p t m b", t=4, b=2),
+        )
+        nc.vector.tensor_copy(out=wsperm[:], in_=wsraw[:].rearrange("p (m t) -> p t m", t=4))
+        wz_i = wz[:].rearrange("p t j c -> p (t j c)").bitcast(I32).rearrange("p (t j c) -> p t j c", t=4, j=4)
+        wperm_i = wperm[:].rearrange("p t c -> p (t c)").bitcast(I32).rearrange("p (t c) -> p t c", t=4)
+        wsp_i = wsp[:].rearrange("p t j c -> p (t j c)").bitcast(I32).rearrange("p (t j c) -> p t j c", t=4, j=4)
+        wsperm_i = wsperm[:].rearrange("p t c -> p (t c)").bitcast(I32).rearrange("p (t c) -> p t c", t=4)
         for j in range(4):
-            nc.vector.tensor_copy(
-                out=wz[:, :, j, 64 * j : 64 * j + 64].rearrange("p t (m b) -> p t m b", b=2),
-                in_=wraw[:].rearrange("p (m t b) -> p t m b", t=4, b=2),
-            )
-            nc.vector.tensor_copy(
-                out=wsp[:, :, j, :], in_=wsraw[:].rearrange("p (m t) -> p t m", t=4)
-            )
+            nc.vector.tensor_copy(out=wz_i[:, :, j, 16 * j : 16 * j + 16], in_=wperm_i)
+            nc.vector.tensor_copy(out=wsp_i[:, :, j, :], in_=wsperm_i)
         affine(1)
         clamp(1)
         interleave(2)
@@ -340,27 +344,22 @@ def tile_neuralbasismodelsharedshapes_x2_kernel(
                 stage2(k - 1)
             quant_u(k + 1, 2 if m == 7 else 1)
             stage1(k + 1)
-            for h in range(2):
-                if (k + 5, h) in V_CHUNKS:
-                    interleave_v(k + 5, h)
-            if m == 6:
-                round_out(0)
             relu_s(k, 0)
             relu_s(k, 1)
-            if m == 6:
-                quant_out(0)
-                store_planes(0)
         relu_s(15, 0)
         quant_q(14)
         stage2(14)
+        relu_s(15, 1)
         quant_q(15, 0, 128)
         stage2(15, (0,))
         copy_out(1, 2)
-        relu_s(15, 1)
         quant_q(15, 128, 256)
         stage2(15, (1,))
         copy_out(1, 3, 2)
+        round_out(0)
         round_out(1, 0, 256)
+        quant_out(0)
+        store_planes(0)
         round_out(1, 256, 512)
         quant_out(1, 0, 256)
         quant_out(1, 256, 512)

@@ -18,6 +18,7 @@ FLOPS = 2 * N * F * H * K + 2 * N * F * K * C
 P = 128
 BIG = 3.0e38
 UNITS = 16
+G_COLS = 800
 N_PE = 2
 SCRATCH = N - UNITS
 
@@ -147,21 +148,19 @@ def tile_neuralbasismodelsharedshapes_x2_kernel(
 
         ys, us, ucs, zs, qs, qcs, acc, of, ob, oqs = {}, {}, {}, {}, {}, {}, {}, {}, {}, {}
 
-        def affine(m, part=None):
+        def affine(m, e=slice(0, 2), c=slice(0, 1024), ts=(0, 1, 2, 3)):
             if m not in ys:
                 y = ypool.tile([P, 2, 4, 1024], BF16, name="y")
                 ys[m] = y
-            e, c = part if part else (slice(0, 2), slice(0, 1024))
-            for t in range(4):
+            for t in ts:
                 nc.vector.tensor_scalar(
                     out=ys[m][:, e, t, c], in0=xb[m][:, e, c], scalar1=ga[:, t : t + 1], scalar2=gb[:, t : t + 1],
                     op0=ALU.mult, op1=ALU.add,
                 )
 
-        def clamp(m, part=None):
-            e, c = part if part else (slice(0, 2), slice(0, 1024))
-            for t in range(4):
-                nc.vector.tensor_scalar(
+        def clamp(m, e=slice(0, 2), c=slice(0, 1024), ts=(0, 1, 2, 3), engine=nc.vector):
+            for t in ts:
+                engine.tensor_scalar(
                     out=ys[m][:, e, t, c], in0=ys[m][:, e, t, c], scalar1=lo[:, t : t + 1], scalar2=hi[:, t : t + 1],
                     op0=ALU.max, op1=ALU.min,
                 )
@@ -265,11 +264,14 @@ def tile_neuralbasismodelsharedshapes_x2_kernel(
                 in_=of[G][:, t, :],
             )
 
-        def round_out(G, c0=0, c1=C):
+        def round_out(G, c0=0, c1=C, copy=nc.vector.tensor_copy):
             if G not in ob:
                 o16 = opool.tile([P, C, 4], BF16, name="o16", align_bytes=64)
                 ob[G] = o16
-            nc.vector.tensor_copy(out=ob[G][:, c0:c1, :], in_=of[G][:, :, c0:c1].rearrange("p t c -> p c t"))
+            copy(
+                out=ob[G][:, c0:c1, :].rearrange("p (c i) t -> p c t i", i=4),
+                in_=of[G][:, :, c0:c1].rearrange("p t (c i) -> p c t i", i=4),
+            )
 
         def quant_out(G, c0=0, c1=C):
             if G not in oqs:
@@ -283,23 +285,24 @@ def tile_neuralbasismodelsharedshapes_x2_kernel(
                 in_=ob[G][:, c0:c1, :].rearrange("p c t -> p (c t)"),
             )
 
-        def store_planes(G):
-            oc, osc = oqs[G]
+        def store_words(G, c0=0, c1=C):
             nc.sync.dma_start(
-                out=out_1[G].rearrange("p m t -> p (m t)").bitcast(I32), in_=oc[:].bitcast(I32)
+                out=out_1[G].rearrange("p m t -> p (m t)").bitcast(I32)[:, c0:c1], in_=oqs[G][0][:, c0:c1].bitcast(I32)
             )
+
+        def store_scales(G, queue):
             for Q in range(4):
-                nc.sync.dma_start(
+                queue.dma_start(
                     out=out_2[G, 4 * Q : 4 * Q + 4, :].bitcast(I32),
-                    in_=osc[32 * Q : 32 * Q + 4, :].bitcast(I32),
+                    in_=oqs[G][1][32 * Q : 32 * Q + 4, :].bitcast(I32),
                 )
 
-        for part in ((0, slice(0, 512)), (0, slice(512, 1024))):
-            affine(0, part)
-            clamp(0, part)
+        for c in (slice(0, 512), slice(512, 1024)):
+            affine(0, 0, c)
+            clamp(0, 0, c)
         interleave(0)
-        affine(0, (1, slice(0, 1024)))
-        clamp(0, (1, slice(0, 1024)))
+        affine(0, 1)
+        clamp(0, 1)
         interleave(1)
         nc.vector.tensor_copy(
             out=wperm[:].rearrange("p t (m b) -> p t m b", b=2),
@@ -320,32 +323,44 @@ def tile_neuralbasismodelsharedshapes_x2_kernel(
 
         for m in range(8):
             k = 2 * m
-            if m + 2 < 8:
-                affine(m + 2)
+            ahead = m + 2 < 8
+            if ahead:
+                affine(m + 2, ts=(0, 1, 2))
             if m > 0:
                 quant_q(k - 2)
                 stage2(k - 2)
             quant_u(k)
             stage1(k)
+            if ahead:
+                affine(m + 2, 0, ts=(3,))
+                if m > 0:
+                    clamp(m + 2, 0, slice(0, G_COLS), (3,), nc.gpsimd)
             if m > 0:
                 relu_s(k - 1, 0)
                 relu_s(k - 1, 1)
-            if m + 2 < 8:
-                clamp(m + 2)
+            if ahead:
+                clamp(m + 2, ts=(0, 1, 2))
+                clamp(m + 2, 0, slice(G_COLS if m > 0 else 0, 1024), (3,))
                 interleave(k + 4)
             if m in (3, 5, 7):
                 G, half = (m - 3) // 4, ((m - 3) // 2) % 2
                 copy_out(G, 2 * half)
                 copy_out(G, 2 * half + 1)
-            if m + 2 < 8:
-                interleave(k + 5)
             if m > 0:
                 quant_q(k - 1)
                 stage2(k - 1)
             quant_u(k + 1, 2 if m == 7 else 1)
             stage1(k + 1)
+            if ahead:
+                affine(m + 2, 1, ts=(3,))
+                clamp(m + 2, 1, slice(0, G_COLS), (3,), nc.gpsimd)
             relu_s(k, 0)
             relu_s(k, 1)
+            if ahead:
+                clamp(m + 2, 1, slice(G_COLS, 1024), (3,))
+                interleave(k + 5)
+            if m == 6:
+                round_out(0, copy=nc.scalar.copy)
         relu_s(15, 0)
         quant_q(14)
         stage2(14)
@@ -356,11 +371,13 @@ def tile_neuralbasismodelsharedshapes_x2_kernel(
         quant_q(15, 128, 256)
         stage2(15, (1,))
         copy_out(1, 3, 2)
-        round_out(0)
-        round_out(1, 0, 256)
         quant_out(0)
-        store_planes(0)
-        round_out(1, 256, 512)
+        store_words(0)
+        store_scales(0, nc.sync)
+        round_out(1, 256, 512, nc.scalar.copy)
+        round_out(1, 0, 256)
         quant_out(1, 0, 256)
+        store_words(1, 0, 256)
         quant_out(1, 256, 512)
-        store_planes(1)
+        store_words(1, 256, 512)
+        store_scales(1, nc.scalar)

@@ -18,7 +18,6 @@ FLOPS = 2 * N * F * H * K + 2 * N * F * K * C
 P = 128
 BIG = 3.0e38
 UNITS = 16
-G_COLS = 800
 N_PE = 2
 SCRATCH = N - UNITS
 
@@ -56,14 +55,14 @@ def tile_neuralbasismodelsharedshapes_x2_kernel(
 
         wraw = keep.tile([P, 2 * K], U8, align_bytes=64)
         wsraw = keep.tile([P, K], U8, align_bytes=64)
-        wz = keep.tile([P, 4, 4, 2 * P], U8, align_bytes=64)
+        wz = keep.tile([P, 4, 5 * 2 * P], U8, align_bytes=64)
         wperm = keep.tile([P, 4, 64], U8, align_bytes=64)
         wsperm = keep.tile([P, 4, 32], U8, align_bytes=64)
         wsp = keep.tile([P, 4, 4, 32], U8, align_bytes=64)
         vt = keep.tile([P, 4, 2 * C], U8, align_bytes=64)
         vs = keep.tile([P, 4, C], U8, align_bytes=64)
         nc.gpsimd.memset(wsraw[:].bitcast(I32), 0)
-        nc.vector.memset(wz[:].rearrange("p t j c -> p (t j c)").bitcast(I32), 0)
+        nc.vector.memset(wz[:].rearrange("p t c -> p (t c)").bitcast(I32), 0)
         nc.gpsimd.memset(vs[:].rearrange("p g n -> p (g n)").bitcast(I32), 0)
         nc.sync.dma_start(out=wraw[:].bitcast(I32), in_=w_words[0].bitcast(I32))
         nc.scalar.dma_start(
@@ -199,7 +198,7 @@ def tile_neuralbasismodelsharedshapes_x2_kernel(
                         cols = slice(512 * tt + 128 * j, 512 * tt + 128 * j + 128)
                         nc.tensor.matmul_mx(
                             out=z[:, t, :],
-                            lhsT=wz[:, t, j, :].bitcast(FP4X4),
+                            lhsT=wz[:, t, 256 * j : 256 * j + 256].bitcast(FP4X4),
                             lhsT_scale=wsp[:, t, :, :].rearrange("p j m -> p (j m)"),
                             rhs=codes[:, cols].bitcast(FP8X4),
                             rhs_scale=scales[:, cols],
@@ -309,13 +308,12 @@ def tile_neuralbasismodelsharedshapes_x2_kernel(
             in_=wraw[:].rearrange("p (m t b) -> p t m b", t=4, b=2),
         )
         nc.vector.tensor_copy(out=wsperm[:], in_=wsraw[:].rearrange("p (m t) -> p t m", t=4))
-        wz_i = wz[:].rearrange("p t j c -> p (t j c)").bitcast(I32).rearrange("p (t j c) -> p t j c", t=4, j=4)
+        wz_i = wz[:].rearrange("p t c -> p (t c)").bitcast(I32).rearrange("p (t j c) -> p t j c", t=4, c=80)
         wperm_i = wperm[:].rearrange("p t c -> p (t c)").bitcast(I32).rearrange("p (t c) -> p t c", t=4)
         wsp_i = wsp[:].rearrange("p t j c -> p (t j c)").bitcast(I32).rearrange("p (t j c) -> p t j c", t=4, j=4)
         wsperm_i = wsperm[:].rearrange("p t c -> p (t c)").bitcast(I32).rearrange("p (t c) -> p t c", t=4)
-        for j in range(4):
-            nc.vector.tensor_copy(out=wz_i[:, :, j, 16 * j : 16 * j + 16], in_=wperm_i)
-            nc.vector.tensor_copy(out=wsp_i[:, :, j, :], in_=wsperm_i)
+        nc.vector.tensor_copy(out=wz_i[:, :, 0:4, 0:16], in_=wperm_i.unsqueeze(2).to_broadcast([P, 4, 4, 16]))
+        nc.vector.tensor_copy(out=wsp_i, in_=wsperm_i.unsqueeze(2).to_broadcast([P, 4, 4, 8]))
         affine(1)
         clamp(1)
         interleave(2)
@@ -325,42 +323,35 @@ def tile_neuralbasismodelsharedshapes_x2_kernel(
             k = 2 * m
             ahead = m + 2 < 8
             if ahead:
-                affine(m + 2, ts=(0, 1, 2))
+                affine(m + 2)
+            if m > 1:
+                quant_q(k - 3)
+                stage2(k - 3)
             if m > 0:
-                quant_q(k - 2)
-                stage2(k - 2)
+                relu_s(k - 2, 0)
+                relu_s(k - 2, 1)
             quant_u(k)
             stage1(k)
             if ahead:
-                affine(m + 2, 0, ts=(3,))
-                if m > 0:
-                    clamp(m + 2, 0, slice(0, G_COLS), (3,), nc.gpsimd)
-            if m > 0:
-                relu_s(k - 1, 0)
-                relu_s(k - 1, 1)
-            if ahead:
-                clamp(m + 2, ts=(0, 1, 2))
-                clamp(m + 2, 0, slice(G_COLS if m > 0 else 0, 1024), (3,))
+                clamp(m + 2)
                 interleave(k + 4)
             if m in (3, 5, 7):
                 G, half = (m - 3) // 4, ((m - 3) // 2) % 2
                 copy_out(G, 2 * half)
                 copy_out(G, 2 * half + 1)
+            if ahead:
+                interleave(k + 5)
             if m > 0:
-                quant_q(k - 1)
-                stage2(k - 1)
+                quant_q(k - 2)
+                stage2(k - 2)
+                relu_s(k - 1, 0)
+                relu_s(k - 1, 1)
             quant_u(k + 1, 2 if m == 7 else 1)
             stage1(k + 1)
-            if ahead:
-                affine(m + 2, 1, ts=(3,))
-                clamp(m + 2, 1, slice(0, G_COLS), (3,), nc.gpsimd)
-            relu_s(k, 0)
-            relu_s(k, 1)
-            if ahead:
-                clamp(m + 2, 1, slice(G_COLS, 1024), (3,))
-                interleave(k + 5)
-            if m == 6:
-                round_out(0, copy=nc.scalar.copy)
+        quant_q(13)
+        stage2(13)
+        relu_s(14, 0)
+        relu_s(14, 1)
         relu_s(15, 0)
         quant_q(14)
         stage2(14)
@@ -371,13 +362,14 @@ def tile_neuralbasismodelsharedshapes_x2_kernel(
         quant_q(15, 128, 256)
         stage2(15, (1,))
         copy_out(1, 3, 2)
+        round_out(0)
+        round_out(1, 384, 512, nc.scalar.copy)
+        round_out(1, 0, 256)
         quant_out(0)
         store_words(0)
         store_scales(0, nc.sync)
-        round_out(1, 256, 512, nc.scalar.copy)
-        round_out(1, 0, 256)
+        round_out(1, 256, 384)
         quant_out(1, 0, 256)
-        store_words(1, 0, 256)
         quant_out(1, 256, 512)
-        store_words(1, 256, 512)
-        store_scales(1, nc.scalar)
+        store_words(1)
+        store_scales(1, nc.sync)

from contextlib import ExitStack

import concourse.mybir as mybir
from concourse.masks import make_identity

F32 = mybir.dt.float32
BF16 = mybir.dt.bfloat16
I32 = mybir.dt.int32
U32 = mybir.dt.uint32
U8 = mybir.dt.uint8
FP8X4 = mybir.dt.float8_e4m3fn_x4
FP4X4 = mybir.dt.float4_e2m1fn_x4
ALU = mybir.AluOpType

N, F, H, K, C = 1024, 16, 512, 128, 512
FLOPS = 2 * N * F * H * K + 2 * N * F * K * C

P = 128
BIG = 3.0e38
UNITS = 16
N_PE = 2
SCRATCH = N - UNITS


def tile_neuralbasismodelsharedshapes_x2_kernel(
    tc, x, a, b, g, w_words, w_scales, s, v_words, v_scales, out_0, out_1, out_2
):
    nc = tc.nc
    with ExitStack() as ctx:
        keep = ctx.enter_context(tc.tile_pool(name="keep", bufs=1))
        xpool = ctx.enter_context(tc.tile_pool(name="xpool", bufs=UNITS // 2))
        ypool = ctx.enter_context(tc.tile_pool(name="ypool", bufs=3))
        upool = ctx.enter_context(tc.tile_pool(name="upool", bufs=5))
        cpool = ctx.enter_context(tc.tile_pool(name="cpool", bufs=3))
        qpool = ctx.enter_context(tc.tile_pool(name="qpool", bufs=3))
        qcpool = ctx.enter_context(tc.tile_pool(name="qcpool", bufs=4))
        opool = ctx.enter_context(tc.tile_pool(name="opool", bufs=2))
        zps = ctx.enter_context(tc.psum_pool(name="zps", bufs=4))
        ops = ctx.enter_context(tc.psum_pool(name="ops", bufs=1))
        ctx.enter_context(tc.manual_schedule())

        xs = keep.tile([P, 2, 4, F], BF16)
        x_view = x.rearrange("(G p t) f -> p G t f", G=2, t=4)
        nc.sync.dma_start(out=xs[:, 0], in_=x_view[:, 0])
        a_sb = keep.tile([P, 4], BF16)
        b_sb = keep.tile([P, 4], BF16)
        g_sb = keep.tile([P, 4], BF16)
        s_sb = keep.tile([P, 4, 4], BF16)
        nc.scalar.dma_start(out=g_sb[:], in_=g.rearrange("(p t) -> p t", t=4))
        nc.scalar.dma_start(out=a_sb[:], in_=a.rearrange("(p t) -> p t", t=4))
        nc.scalar.dma_start(out=b_sb[:], in_=b.rearrange("(p t) -> p t", t=4))
        nc.sync.dma_start(out=xs[:, 1], in_=x_view[:, 1])
        ident = keep.tile([P, P], BF16)
        make_identity(nc, ident[:])

        wraw = keep.tile([P, 2 * K], U8, align_bytes=64)
        wsraw = keep.tile([P, K], U8, align_bytes=64)
        wz = keep.tile([P, 4, 5 * 2 * P], U8, align_bytes=64)
        wperm = keep.tile([P, 4, 64], U8, align_bytes=64)
        wsperm = keep.tile([P, 4, 32], U8, align_bytes=64)
        wsp = keep.tile([P, 4, 4, 32], U8, align_bytes=64)
        vt = keep.tile([P, 4, 2 * C], U8, align_bytes=64)
        vs = keep.tile([P, 4, C], U8, align_bytes=64)
        nc.gpsimd.memset(wsraw[:].bitcast(I32), 0)
        nc.vector.memset(wz[:].rearrange("p t c -> p (t c)").bitcast(I32), 0)
        nc.gpsimd.memset(vs[:].rearrange("p g n -> p (g n)").bitcast(I32), 0)
        nc.sync.dma_start(out=wraw[:].bitcast(I32), in_=w_words[0].bitcast(I32))
        nc.scalar.dma_start(
            out=s_sb[:], in_=s.rearrange("f k -> (f k)").rearrange("(g p t) -> p g t", p=P, t=4)
        )
        for Q in range(4):
            nc.sync.dma_start(
                out=wsraw[32 * Q : 32 * Q + 4, :].bitcast(I32),
                in_=w_scales[0, 4 * Q : 4 * Q + 4, :].bitcast(I32),
            )

        ga = keep.tile([P, 4], F32)
        gb = keep.tile([P, 4], F32)
        lo = keep.tile([P, 4], F32)
        hi = keep.tile([P, 4], F32)
        nc.vector.tensor_scalar(out=lo[:], in0=g_sb[:], scalar1=0.0, scalar2=-BIG, op0=ALU.is_lt, op1=ALU.mult)
        nc.vector.tensor_scalar(out=hi[:], in0=g_sb[:], scalar1=0.0, scalar2=BIG, op0=ALU.is_gt, op1=ALU.mult)
        nc.vector.tensor_tensor(out=ga[:], in0=g_sb[:], in1=a_sb[:], op=ALU.mult)
        nc.vector.tensor_tensor(out=gb[:], in0=g_sb[:], in1=b_sb[:], op=ALU.mult)

        def unit(u):
            return u // 8, (u // 4) % 2, u % 4

        xp = keep.tile([P, 2, 2, 4, 2, 4], BF16)
        for G in range(2):
            for half in range(2):
                nc.gpsimd.tensor_copy(
                    out=xp[:, G, half],
                    in_=xs[:, G, 2 * half : 2 * half + 2, :].rearrange("p t (g j) -> p g t j", j=4),
                )
        park = out_0[SCRATCH:N, :].bitcast(BF16)

        def park_x():
            zt = zps.tile([P, P], BF16, tag="z", name="zt")
            nc.tensor.transpose(zt[:], xp[:].rearrange("p G h g t j -> p (G h g t j)"), ident[:])
            xt = keep.tile([P, P], BF16)
            nc.scalar.copy(out=xt[:], in_=zt[:])
            nc.sync.dma_start(out=park.rearrange("u (c n) -> (u c) n", n=P), in_=xt[:])

        xb = []
        for m in range(N_PE):
            xu = xpool.tile([P, 2, 1024], BF16, tag="xu", name="xu")
            xb.append(xu)
            for e in range(2):
                G, half, gg = unit(2 * m + e)
                zx = zps.tile([P, 2, 4, P], BF16, tag="z", name="zx")
                for tt in range(2):
                    for j in range(4):
                        f = 4 * gg + j
                        nc.tensor.transpose(
                            zx[:, tt, j, :],
                            xs[:, G, 2 * half + tt, f : f + 1].to_broadcast([P, P]),
                            ident[:],
                        )
                parts = 2 if (m, e) == (0, 0) else 1
                w = 1024 // parts
                for i in range(parts):
                    nc.scalar.copy(
                        out=xu[:, e, w * i : w * i + w],
                        in_=zx[:].rearrange("p t j n -> p (t j n)")[:, w * i : w * i + w],
                    )
                if (m, e) == (0, 0):
                    park_x()

        for m in range(N_PE, UNITS // 2):
            xu = xpool.tile([P, 2, 1024], BF16, tag="xu", name="xu")
            nc.sync.dma_start(
                out=xu[:].rearrange("p e c -> p (e c)"),
                in_=park[2 * m : 2 * m + 2, :].rearrange("u c -> (u c)").partition_broadcast(P),
            )
            xb.append(xu)

        nc.sync.dma_start(
            out=vt[:].rearrange("p g n -> p (g n)").bitcast(I32).rearrange("p (g n) -> p g n", g=4),
            in_=v_words.bitcast(I32).rearrange("g p n -> p g n"),
        )
        for Q in range(4):
            nc.sync.dma_start(
                out=vs[32 * Q : 32 * Q + 4, :, :].rearrange("p g n -> p (g n)").bitcast(I32).rearrange("p (g n) -> p g n", g=4),
                in_=v_scales.bitcast(I32)[:, 4 * Q : 4 * Q + 4, :].rearrange("g r n -> r g n"),
            )

        ys, us, ucs, zs, qs, qcs, acc, of, ob, oqs = {}, {}, {}, {}, {}, {}, {}, {}, {}, {}

        def affine(m, e=slice(0, 2), c=slice(0, 1024), ts=(0, 1, 2, 3)):
            if m not in ys:
                y = ypool.tile([P, 2, 4, 1024], BF16, name="y")
                ys[m] = y
            for t in ts:
                nc.vector.tensor_scalar(
                    out=ys[m][:, e, t, c], in0=xb[m][:, e, c], scalar1=ga[:, t : t + 1], scalar2=gb[:, t : t + 1],
                    op0=ALU.mult, op1=ALU.add,
                )

        def clamp(m, e=slice(0, 2), c=slice(0, 1024), ts=(0, 1, 2, 3), engine=nc.vector):
            for t in ts:
                engine.tensor_scalar(
                    out=ys[m][:, e, t, c], in0=ys[m][:, e, t, c], scalar1=lo[:, t : t + 1], scalar2=hi[:, t : t + 1],
                    op0=ALU.max, op1=ALU.min,
                )

        def interleave(k):
            u = upool.tile([P, 1024, 4], BF16, name="u", align_bytes=64)
            us[k] = u
            y = ys[k // 2]
            for h in range(2):
                y0 = 512 * h
                nc.scalar.copy(
                    out=u[:, 512 * h : 512 * h + 512, :].rearrange("p (c i) t -> p c t i", i=4),
                    in_=y[:, k % 2, :, y0 : y0 + 512].rearrange("p t (c i) -> p c t i", i=4),
                )

        def quant_u(k, parts=1):
            codes = cpool.tile([P, 1024], U32, name="codes", align_bytes=64)
            scales = cpool.tile([P, 1024], U8, name="scales", align_bytes=64)
            ucs[k] = (codes, scales)
            w = 1024 // parts
            for i in range(parts):
                cols = slice(w * i, w * i + w)
                nc.vector.quantize_mx(
                    out=codes[:, cols].bitcast(FP8X4),
                    scales=scales[:, cols],
                    in_=us[k][:, cols, :].rearrange("p c t -> p (c t)"),
                )

        def stage1(k):
            codes, scales = ucs[k]
            for tt in range(2):
                z = zps.tile([P, 4, P], F32, tag="z", name="z")
                zs[k, tt] = z
                for t in range(4):
                    for j in range(4):
                        cols = slice(512 * tt + 128 * j, 512 * tt + 128 * j + 128)
                        nc.tensor.matmul_mx(
                            out=z[:, t, :],
                            lhsT=wz[:, t, 256 * j : 256 * j + 256].bitcast(FP4X4),
                            lhsT_scale=wsp[:, t, :, :].rearrange("p j m -> p (j m)"),
                            rhs=codes[:, cols].bitcast(FP8X4),
                            rhs_scale=scales[:, cols],
                            start=(j == 0),
                            stop=(j == 3),
                        )

        def relu_s(k, tt):
            gg = unit(k)[2]
            if tt == 0:
                q = qpool.tile([P, 256, 4], BF16, name="q", align_bytes=64)
                qs[k] = q
            nc.vector.scalar_tensor_tensor(
                out=qs[k][:, 128 * tt : 128 * tt + 128, :],
                in0=zs[k, tt][:].rearrange("p t n -> p n t"),
                scalar=0.0,
                in1=s_sb[:, gg, :].unsqueeze(1).to_broadcast([P, P, 4]),
                op0=ALU.max,
                op1=ALU.mult,
            )

        def quant_q(k, n0=0, n1=256):
            if k not in qcs:
                qc = qcpool.tile([P, 256], U32, name="qc", align_bytes=64)
                qsc = qcpool.tile([P, 256], U8, name="qsc", align_bytes=64)
                qcs[k] = (qc, qsc)
            qc, qsc = qcs[k]
            nc.vector.quantize_mx(
                out=qc[:, n0:n1].bitcast(FP8X4),
                scales=qsc[:, n0:n1],
                in_=qs[k][:, n0:n1, :].rearrange("p c t -> p (c t)"),
            )

        def stage2(k, tts=(0, 1)):
            G, half, gg = unit(k)
            qc, qsc = qcs[k]
            for tt in tts:
                t = 2 * half + tt
                if gg == 0:
                    o = ops.tile([P, C], F32, tag="o%d" % t, name="o")
                    acc[G, t] = o
                cols = slice(128 * tt, 128 * tt + 128)
                nc.tensor.matmul_mx(
                    out=acc[G, t][:],
                    lhsT=qc[:, cols].bitcast(FP8X4),
                    lhsT_scale=qsc[:, cols],
                    rhs=vt[:, gg, :].bitcast(FP4X4),
                    rhs_scale=vs[:, gg, :],
                    start=(gg == 0),
                    stop=(gg == 3),
                )

        def copy_out(G, t, parts=1):
            if t == 0:
                o32 = opool.tile([P, 4, C], F32, name="o32")
                of[G] = o32
            w = C // parts
            for i in range(parts):
                nc.scalar.copy(out=of[G][:, t, w * i : w * i + w], in_=acc[G, t][:, w * i : w * i + w])
            nc.sync.dma_start(
                out=out_0[512 * G : 512 * G + 512, :].rearrange("(p t) c -> p t c", t=4)[:, t, :],
                in_=of[G][:, t, :],
            )

        def round_out(G, c0=0, c1=C, copy=nc.vector.tensor_copy):
            if G not in ob:
                o16 = opool.tile([P, C, 4], BF16, name="o16", align_bytes=64)
                ob[G] = o16
            copy(
                out=ob[G][:, c0:c1, :].rearrange("p (c i) t -> p c t i", i=4),
                in_=of[G][:, :, c0:c1].rearrange("p t (c i) -> p c t i", i=4),
            )

        def quant_out(G, c0=0, c1=C):
            if G not in oqs:
                oc = opool.tile([P, C], U32, name="oc", align_bytes=64)
                osc = opool.tile([P, C], U8, name="osc", align_bytes=64)
                oqs[G] = (oc, osc)
            oc, osc = oqs[G]
            nc.vector.quantize_mx(
                out=oc[:, c0:c1].bitcast(FP8X4),
                scales=osc[:, c0:c1],
                in_=ob[G][:, c0:c1, :].rearrange("p c t -> p (c t)"),
            )

        def store_words(G, c0=0, c1=C):
            nc.sync.dma_start(
                out=out_1[G].rearrange("p m t -> p (m t)").bitcast(I32)[:, c0:c1], in_=oqs[G][0][:, c0:c1].bitcast(I32)
            )

        def store_scales(G, queue):
            for Q in range(4):
                queue.dma_start(
                    out=out_2[G, 4 * Q : 4 * Q + 4, :].bitcast(I32),
                    in_=oqs[G][1][32 * Q : 32 * Q + 4, :].bitcast(I32),
                )

        for c in (slice(0, 512), slice(512, 1024)):
            affine(0, 0, c)
            clamp(0, 0, c)
        interleave(0)
        affine(0, 1)
        clamp(0, 1)
        interleave(1)
        nc.vector.tensor_copy(
            out=wperm[:].rearrange("p t (m b) -> p t m b", b=2),
            in_=wraw[:].rearrange("p (m t b) -> p t m b", t=4, b=2),
        )
        nc.vector.tensor_copy(out=wsperm[:], in_=wsraw[:].rearrange("p (m t) -> p t m", t=4))
        wz_i = wz[:].rearrange("p t c -> p (t c)").bitcast(I32).rearrange("p (t j c) -> p t j c", t=4, c=80)
        wperm_i = wperm[:].rearrange("p t c -> p (t c)").bitcast(I32).rearrange("p (t c) -> p t c", t=4)
        wsp_i = wsp[:].rearrange("p t j c -> p (t j c)").bitcast(I32).rearrange("p (t j c) -> p t j c", t=4, j=4)
        wsperm_i = wsperm[:].rearrange("p t c -> p (t c)").bitcast(I32).rearrange("p (t c) -> p t c", t=4)
        nc.vector.tensor_copy(out=wz_i[:, :, 0:4, 0:16], in_=wperm_i.unsqueeze(2).to_broadcast([P, 4, 4, 16]))
        nc.vector.tensor_copy(out=wsp_i, in_=wsperm_i.unsqueeze(2).to_broadcast([P, 4, 4, 8]))
        affine(1)
        clamp(1)
        interleave(2)
        interleave(3)

        for m in range(8):
            k = 2 * m
            ahead = m + 2 < 8
            if ahead:
                affine(m + 2)
            if m > 1:
                quant_q(k - 3)
                stage2(k - 3)
            if m > 0:
                relu_s(k - 2, 0)
                relu_s(k - 2, 1)
            quant_u(k)
            stage1(k)
            if ahead:
                clamp(m + 2)
                interleave(k + 4)
            if m in (3, 5, 7):
                G, half = (m - 3) // 4, ((m - 3) // 2) % 2
                copy_out(G, 2 * half)
                copy_out(G, 2 * half + 1)
            if ahead:
                interleave(k + 5)
            if m > 0:
                quant_q(k - 2)
                stage2(k - 2)
                relu_s(k - 1, 0)
                relu_s(k - 1, 1)
            quant_u(k + 1, 2 if m == 7 else 1)
            stage1(k + 1)
        quant_q(13)
        stage2(13)
        relu_s(14, 0)
        relu_s(14, 1)
        relu_s(15, 0)
        quant_q(14)
        stage2(14)
        relu_s(15, 1)
        quant_q(15, 0, 128)
        stage2(15, (0,))
        copy_out(1, 2)
        quant_q(15, 128, 256)
        stage2(15, (1,))
        copy_out(1, 3, 2)
        round_out(0)
        round_out(1, 384, 512, nc.scalar.copy)
        round_out(1, 0, 256)
        quant_out(0)
        store_words(0)
        store_scales(0, nc.sync)
        round_out(1, 256, 384)
        quant_out(1, 0, 256)
        quant_out(1, 256, 512)
        store_words(1)
        store_scales(1, nc.sync)
